import numpy as np
import ml_dtypes


def mxq(x, axis, fmt="e4m3"):
    dtype, down = {"e4m3": (ml_dtypes.float8_e4m3fn, 7), "e5m2": (ml_dtypes.float8_e5m2, 14)}[fmt]
    v = np.moveaxis(np.asarray(x, np.float32).astype(ml_dtypes.bfloat16).astype(np.float64), axis, -1)
    blocks = v.reshape(v.shape[:-1] + (-1, 32))
    amax = np.abs(blocks).max(-1, keepdims=True)
    byte = np.maximum(np.where(amax > 0, np.frexp(amax)[1] - 1 + 127, 0) - down, 1)
    scale = np.exp2(byte - 127.0)
    codes = (blocks / scale).astype(np.float32).astype(dtype).astype(np.float64)
    return np.moveaxis((codes * scale).reshape(v.shape), -1, axis)


WIDE = False


def mx_kscale(k):
    if not WIDE:
        return np.ones(k)
    levels = np.array([10, -10, 5, -5, 0])
    if k % 512:
        return np.exp2(np.random.permutation(np.resize(levels, k // 32))).repeat(32)
    a = np.empty((k // 512, 16))
    for p in range(k // 512):
        a[p, :8] = np.random.permutation(np.resize(levels, 8))
        for g in range(8):
            far = levels[np.abs(levels - a[p, g]) >= 10]
            a[p, g + 8] = far[np.random.randint(len(far))]
    return np.exp2(a.ravel()).repeat(32)


def f64(x):
    return np.asarray(x).astype(np.float64)


def striped(idx):
    return np.tile(idx.reshape(-1, 16).T, (8, 1)).astype(np.uint16)


def unstriped(offs):
    return offs[:16].T.reshape(-1).astype(np.int64)


def sigmoid(v):
    return 1.0 / (1.0 + np.exp(-np.maximum(v, -700.0)))


K, T, E, C, H, N = 1024, 1024, 4, 128, 512, 128


def by_expert(wq, xq):
    return np.concatenate([wq[e].T @ xq[:, e * C:(e + 1) * C] for e in range(E)], axis=1)


def setup_inputs():
    n = np.random.standard_normal
    s = mx_kscale(K)[:, None]
    u = mx_kscale(H)
    return {
        "xT": (n((K, T)) * s).astype(np.float32),
        "xr": n((N, T)).astype(np.float32),
        "w1": (n((E, K, H)) / np.sqrt(K) / s[None]).astype(np.float32),
        "w3": (n((E, K, H)) / np.sqrt(K) / s[None] * u[None, None, :]).astype(np.float32),
        "w2": (n((E, H, N)) / np.sqrt(H) / u[None, :, None]).astype(np.float32),
        "gate": np.tile(np.random.uniform(0.2, 1.0, E * C), (N, 1)).astype(np.float32),
        "offs": striped(np.random.permutation(T)[:E * C]),
    }


def reference(xT, xr, w1, w3, w2, gate, offs):
    idx = unstriped(offs)
    xq = mxq(f64(xT)[:, idx], 0, "e4m3")
    h = sigmoid(by_expert(mxq(f64(w1), 1, "e4m3"), xq))
    h = h * by_expert(mxq(f64(w3), 1, "e4m3"), xq)
    y = by_expert(mxq(f64(w2), 1, "e4m3"), mxq(h, 0, "e4m3"))
    out = f64(xr).copy()
    out[:, idx] += f64(gate) * y
    return out

@@ -1,0 +1,241 @@
+from contextlib import ExitStack
+
+import concourse.mybir as mybir
+
+K, T, E, C, H, N = 1024, 1024, 4, 128, 512, 128
+FLOPS = 2 * E * C * (2 * K * H + H * N)
+
+F32 = mybir.dt.float32
+BF16 = mybir.dt.bfloat16
+U32 = mybir.dt.uint32
+U16 = mybir.dt.uint16
+U8 = mybir.dt.uint8
+FP8X4 = mybir.dt.float8_e4m3fn_x4
+SIGMOID = mybir.ActivationFunctionType.Sigmoid
+ADD, MULT = mybir.AluOpType.add, mybir.AluOpType.mult
+
+P = 128
+PACK = 4
+PASSES = K // (P * PACK)
+X_PIECES = ((0, 0, 256), (0, 256, 256), (0, 512, 512), (1, 0, 512), (1, 512, 512))
+X_VECTOR = 4 / 16
+M_VECTOR = 60
+M_VECTOR_LAST = 80
+OUT_PIECES = ((0, 512), (512, 256), (768, 256))
+LIST_COLUMNS = C // 16
+
+
+def tile_moe_res_glu_sigmoid_kernel(tc, xT, xr, w1, w3, w2, gate, offs, out):
+    nc = tc.nc
+    with ExitStack() as ctx:
+        keep = ctx.enter_context(tc.tile_pool(name="keep", bufs=1))
+        xpool = ctx.enter_context(tc.tile_pool(name="xpool", bufs=2))
+        wraw = ctx.enter_context(tc.tile_pool(name="wraw", bufs=12))
+        stage = ctx.enter_context(tc.tile_pool(name="stage", bufs=2))
+        coded = ctx.enter_context(tc.tile_pool(name="coded", bufs=8))
+        small = ctx.enter_context(tc.tile_pool(name="small", bufs=2))
+        psum = ctx.enter_context(tc.psum_pool(name="psum", bufs=2))
+
+        slots = keep.tile([P, E * LIST_COLUMNS], U16, name="slots")
+        x_words = [keep.tile([P, T], U32, name=f"x_words{g}", align_bytes=64) for g in range(PASSES)]
+        x_bytes = [keep.tile([P, T], U8, name=f"x_bytes{g}", align_bytes=64) for g in range(PASSES)]
+        g_words = [keep.tile([P, E * C], U32, name=f"g_words{g}", align_bytes=64) for g in range(PASSES)]
+        g_bytes = [keep.tile([P, E * C], U8, name=f"g_bytes{g}", align_bytes=64) for g in range(PASSES)]
+        scattered = keep.tile([P, T], F32, name="scattered")
+        residual = keep.tile([P, T], F32, name="residual")
+        gates = keep.tile([P, E * C], F32, name="gates")
+        w2_raw = keep.tile([P, E, PACK, N], F32, name="w2_raw")
+        result = keep.tile([P, T], F32, name="result")
+        warm = keep.tile([P, 8], F32, name="warm")
+
+        nc.vector.memset(warm[:], 0.0)
+        nc.scalar.activation(warm[:], warm[:], SIGMOID)
+        for g in range(PASSES):
+            nc.gpsimd.memset(x_bytes[g][:], 0)
+        nc.gpsimd.memset(scattered[:], 0.0)
+
+        x_rows = xT.rearrange("(g p j) t -> g p j t", g=PASSES, j=PACK)
+        x_raw = {}
+        for i, (g, start, width) in enumerate(X_PIECES):
+            x_raw[i] = keep.tile([P, PACK, width], F32, name=f"x_raw{i}")
+            nc.sync.dma_start(x_raw[i][:], x_rows[g, :, :, start : start + width])
+            if i == 0:
+                nc.sync.dma_start(slots[:], offs)
+
+        w2_rows = w2.rearrange("e (p j) n -> p e j n", j=PACK)
+        w_raw = {}
+
+        def load_w(e, which):
+            rows = (w1, w3)[which][e].rearrange("(g p j) c -> g p j c", g=PASSES, j=PACK)
+            for g in range(PASSES):
+                raw = wraw.tile([P, PACK, H], F32, name="w_raw")
+                nc.sync.dma_start(raw[:], rows[g])
+                w_raw[e, which, g] = raw
+
+        for e in range(E):
+            load_w(e, 0)
+            load_w(e, 1)
+            if e == 0:
+                nc.sync.dma_start(w2_raw[:, : E - 1], w2_rows[:, : E - 1])
+                nc.sync.dma_start(gates[:], gate)
+        nc.sync.dma_start(w2_raw[:, E - 1], w2_rows[:, E - 1])
+        nc.sync.dma_start(residual[:], xr)
+
+        def interleave_x(i):
+            width = X_PIECES[i][2]
+            staged = xpool.tile([P, width * PACK], BF16, name="x_staged", align_bytes=64)
+            dst = staged[:].rearrange("p (c i j) -> p c j i", i=4, j=PACK)
+            source = x_raw[i][:].rearrange("p j (c i) -> p c j i", i=4)
+            cut = int(width * X_VECTOR) // 4
+            nc.vector.tensor_copy(dst[:, :cut], source[:, :cut])
+            nc.scalar.copy(dst[:, cut:], source[:, cut:])
+            return staged
+
+        def quantize_x(i, staged):
+            g, start, width = X_PIECES[i]
+            cols = slice(start, start + width)
+            nc.vector.quantize_mx(x_words[g][:, cols].bitcast(FP8X4), x_bytes[g][:, cols], staged[:])
+
+        def interleave_w(e, which, g, cut):
+            staged = stage.tile([P, H * PACK], BF16, name="w_staged", align_bytes=64)
+            dst = staged[:].rearrange("p (t m j) -> p m t j", t=4, j=PACK)
+            source = w_raw[e, which, g][:].rearrange("p j (m t) -> p m t j", t=4)
+            nc.vector.tensor_copy(dst[:, :cut], source[:, :cut])
+            nc.scalar.copy(dst[:, cut:], source[:, cut:])
+            return staged
+
+        w_coded = {}
+
+        def quantize_w(e, which, g, staged):
+            words = coded.tile([P, H], U32, name="w_words", align_bytes=64)
+            scales = coded.tile([P, H], U8, name="w_scales", align_bytes=64)
+            nc.vector.quantize_mx(words[:].bitcast(FP8X4), scales[:], staged[:])
+            w_coded[e, which, g] = (words, scales)
+
+        def products(e, which):
+            bank = psum.tile([P, 4 * C], F32, name=("bank_a", "bank_u")[which])
+            cols = slice(e * C, (e + 1) * C)
+            for t in range(4):
+                chans = slice(t * P, (t + 1) * P)
+                for g in range(PASSES):
+                    words, scales = w_coded[e, which, g]
+                    nc.tensor.matmul_mx(
+                        bank[:, t * C : (t + 1) * C],
+                        lhsT=words[:, chans].bitcast(FP8X4),
+                        lhsT_scale=scales[:, chans],
+                        rhs=g_words[g][:, cols].bitcast(FP8X4),
+                        rhs_scale=g_bytes[g][:, cols],
+                        start=(g == 0),
+                        stop=(g == PASSES - 1),
+                    )
+            return bank
+
+        def gather_words(g):
+            nc.vector.tensor_copy(g_words[g][:], x_words[g][:].indirect(slots[:]))
+
+        def gather_bytes(g):
+            nc.vector.tensor_copy(g_bytes[g][:], x_bytes[g][:].indirect(slots[:]))
+
+        sig, gated, h_coded, w2_coded, ys, bank_u = {}, {}, {}, {}, {}, {}
+
+        def first(e):
+            bank = products(e, 0)
+            sig[e] = small.tile([P, 4 * C], F32, name="sig")
+            nc.scalar.activation(sig[e][:], bank[:], SIGMOID)
+
+        def second(e):
+            bank_u[e] = products(e, 1)
+
+        def gating(e):
+            gated[e] = small.tile([P, 4 * C], BF16, name="gated", align_bytes=64)
+            nc.vector.tensor_tensor(
+                gated[e][:].rearrange("p (n t) -> p n t", t=4),
+                bank_u[e][:].rearrange("p (t n) -> p n t", t=4),
+                sig[e][:].rearrange("p (t n) -> p n t", t=4),
+                MULT,
+            )
+
+        def quantize_h(e):
+            words = small.tile([P, C], U32, name="h_words", align_bytes=64)
+            scales = small.tile([P, C], U8, name="h_scales", align_bytes=64)
+            nc.vector.quantize_mx(words[:].bitcast(FP8X4), scales[:], gated[e][:])
+            h_coded[e] = (words, scales)
+
+        w2_staged = {}
+
+        def interleave_w2(e):
+            w2_staged[e] = small.tile([P, N * PACK], BF16, name="w2_staged", align_bytes=64)
+            dst = w2_staged[e][:].rearrange("p (c i j) -> p c j i", i=4, j=PACK)
+            nc.scalar.copy(dst, w2_raw[:, e].rearrange("p j (c i) -> p c j i", i=4))
+
+        def quantize_w2(e):
+            words = small.tile([P, N], U32, name="w2_words", align_bytes=64)
+            scales = small.tile([P, N], U8, name="w2_scales", align_bytes=64)
+            nc.vector.quantize_mx(words[:].bitcast(FP8X4), scales[:], w2_staged[e][:])
+            w2_coded[e] = (words, scales)
+
+        def down(e):
+            bank = psum.tile([P, C], F32, name="bank_y")
+            nc.tensor.matmul_mx(
+                bank[:],
+                lhsT=w2_coded[e][0][:].bitcast(FP8X4),
+                lhsT_scale=w2_coded[e][1][:],
+                rhs=h_coded[e][0][:].bitcast(FP8X4),
+                rhs_scale=h_coded[e][1][:],
+                start=True,
+                stop=True,
+            )
+            ys[e] = small.tile([P, C], F32, name="y")
+            nc.scalar.copy(ys[e][:], bank[:])
+
+        def scatter(e):
+            window = scattered[:].indirect(slots[:, e * LIST_COLUMNS : (e + 1) * LIST_COLUMNS])
+            nc.vector.tensor_tensor(window, ys[e][:], gates[:, e * C : (e + 1) * C], MULT)
+
+        last_x = None
+        for i in range(len(X_PIECES)):
+            staged = interleave_x(i)
+            if last_x:
+                quantize_x(*last_x)
+            last_x = (i, staged)
+            if i == 4:
+                gather_words(0)
+                gather_bytes(0)
+        pending = None
+        for k in range(16):
+            e, which, g = k // 4, (k // 2) % 2, k % 2
+            step = k % 4
+            if k > 1:
+                quantize_w(*pending)
+            staged = interleave_w(e, which, g, M_VECTOR_LAST if k == 15 else M_VECTOR)
+            if k == 0:
+                quantize_x(*last_x)
+                gather_words(1)
+            if k == 1:
+                quantize_w(*pending)
+                gather_bytes(1)
+            if step == 3:
+                first(e)
+            if e > 0 and step == 0:
+                second(e - 1)
+                interleave_w2(e - 1)
+                gating(e - 1)
+            if e > 0 and step == 1:
+                quantize_h(e - 1)
+                quantize_w2(e - 1)
+                down(e - 1)
+                scatter(e - 1)
+            pending = (e, which, g, staged)
+        e = E - 1
+        quantize_w(*pending)
+        interleave_w2(e)
+        second(e)
+        quantize_w2(e)
+        gating(e)
+        quantize_h(e)
+        down(e)
+        scatter(e)
+        for start, width in OUT_PIECES:
+            cols = slice(start, start + width)
+            nc.vector.tensor_tensor(result[:, cols], scattered[:, cols], residual[:, cols], ADD)
+            nc.sync.dma_start(out[:, cols], result[:, cols])

@@ -19,8 +19,8 @@ PACK = 4
 PASSES = K // (P * PACK)
 X_PIECES = ((0, 0, 256), (0, 256, 256), (0, 512, 512), (1, 0, 512), (1, 512, 512))
 X_VECTOR = 4 / 16
-M_VECTOR = 60
-M_VECTOR_LAST = 80
+T_VECTOR = 2
+T_VECTOR_LAST = 3
 OUT_PIECES = ((0, 512), (512, 256), (768, 256))
 LIST_COLUMNS = C // 16
 
@@ -31,27 +31,30 @@ def tile_moe_res_glu_sigmoid_kernel(tc, xT, xr, w1, w3, w2, gate, offs, out):
         keep = ctx.enter_context(tc.tile_pool(name="keep", bufs=1))
         xpool = ctx.enter_context(tc.tile_pool(name="xpool", bufs=2))
         wraw = ctx.enter_context(tc.tile_pool(name="wraw", bufs=12))
-        stage = ctx.enter_context(tc.tile_pool(name="stage", bufs=2))
+        stage = ctx.enter_context(tc.tile_pool(name="stage", bufs=3))
         coded = ctx.enter_context(tc.tile_pool(name="coded", bufs=8))
         small = ctx.enter_context(tc.tile_pool(name="small", bufs=2))
         psum = ctx.enter_context(tc.psum_pool(name="psum", bufs=2))
 
         slots = keep.tile([P, E * LIST_COLUMNS], U16, name="slots")
         x_words = [keep.tile([P, T], U32, name=f"x_words{g}", align_bytes=64) for g in range(PASSES)]
-        x_bytes = [keep.tile([P, T], U8, name=f"x_bytes{g}", align_bytes=64) for g in range(PASSES)]
+        x_bytes = keep.tile([P, T], U8, name="x_bytes", align_bytes=64)
         g_words = [keep.tile([P, E * C], U32, name=f"g_words{g}", align_bytes=64) for g in range(PASSES)]
-        g_bytes = [keep.tile([P, E * C], U8, name=f"g_bytes{g}", align_bytes=64) for g in range(PASSES)]
+        g_bytes = keep.tile([P, E * C], U8, name="g_bytes", align_bytes=64)
         scattered = keep.tile([P, T], F32, name="scattered")
         residual = keep.tile([P, T], F32, name="residual")
         gates = keep.tile([P, E * C], F32, name="gates")
         w2_raw = keep.tile([P, E, PACK, N], F32, name="w2_raw")
+        w2_staged = keep.tile([P, E, N * PACK], BF16, name="w2_staged", align_bytes=64)
+        w2_words = keep.tile([P, E * N], U32, name="w2_words", align_bytes=64)
+        w2_scales = keep.tile([P, E * N], U8, name="w2_scales", align_bytes=64)
+        weighted = keep.tile([P, E * C], F32, name="weighted")
         result = keep.tile([P, T], F32, name="result")
         warm = keep.tile([P, 8], F32, name="warm")
 
         nc.vector.memset(warm[:], 0.0)
         nc.scalar.activation(warm[:], warm[:], SIGMOID)
-        for g in range(PASSES):
-            nc.gpsimd.memset(x_bytes[g][:], 0)
+        nc.gpsimd.memset(x_bytes[:], 0)
         nc.gpsimd.memset(scattered[:], 0.0)
 
         x_rows = xT.rearrange("(g p j) t -> g p j t", g=PASSES, j=PACK)
@@ -64,18 +67,13 @@ def tile_moe_res_glu_sigmoid_kernel(tc, xT, xr, w1, w3, w2, gate, offs, out):
 
         w2_rows = w2.rearrange("e (p j) n -> p e j n", j=PACK)
         w_raw = {}
-
-        def load_w(e, which):
+        for i in range(2 * E):
+            e, which = i // 2, i % 2
             rows = (w1, w3)[which][e].rearrange("(g p j) c -> g p j c", g=PASSES, j=PACK)
             for g in range(PASSES):
-                raw = wraw.tile([P, PACK, H], F32, name="w_raw")
-                nc.sync.dma_start(raw[:], rows[g])
-                w_raw[e, which, g] = raw
-
-        for e in range(E):
-            load_w(e, 0)
-            load_w(e, 1)
-            if e == 0:
+                w_raw[i, g] = wraw.tile([P, PACK, H], F32, name="w_raw")
+                nc.sync.dma_start(w_raw[i, g][:], rows[g])
+            if i == 1:
                 nc.sync.dma_start(w2_raw[:, : E - 1], w2_rows[:, : E - 1])
                 nc.sync.dma_start(gates[:], gate)
         nc.sync.dma_start(w2_raw[:, E - 1], w2_rows[:, E - 1])
@@ -94,23 +92,23 @@ def tile_moe_res_glu_sigmoid_kernel(tc, xT, xr, w1, w3, w2, gate, offs, out):
         def quantize_x(i, staged):
             g, start, width = X_PIECES[i]
             cols = slice(start, start + width)
-            nc.vector.quantize_mx(x_words[g][:, cols].bitcast(FP8X4), x_bytes[g][:, cols], staged[:])
-
-        def interleave_w(e, which, g, cut):
-            staged = stage.tile([P, H * PACK], BF16, name="w_staged", align_bytes=64)
-            dst = staged[:].rearrange("p (t m j) -> p m t j", t=4, j=PACK)
-            source = w_raw[e, which, g][:].rearrange("p j (m t) -> p m t j", t=4)
-            nc.vector.tensor_copy(dst[:, :cut], source[:, :cut])
-            nc.scalar.copy(dst[:, cut:], source[:, cut:])
-            return staged
+            nc.vector.quantize_mx(x_words[g][:, cols].bitcast(FP8X4), x_bytes[4 * g :, cols], staged[:])
 
         w_coded = {}
 
-        def quantize_w(e, which, g, staged):
+        def interleave_w(i, g, cut):
+            staged = stage.tile([P, H * PACK], BF16, name="w_staged", align_bytes=64)
+            dst = staged[:].rearrange("p (t m j) -> p m j t", t=4, j=PACK)
+            source = w_raw[i, g][:].rearrange("p j (m t) -> p m j t", t=4)
+            nc.vector.tensor_copy(dst[:, :, :, :cut], source[:, :, :, :cut])
+            nc.scalar.copy(dst[:, :, :, cut:], source[:, :, :, cut:])
+            return staged
+
+        def quantize_w(i, g, staged):
             words = coded.tile([P, H], U32, name="w_words", align_bytes=64)
             scales = coded.tile([P, H], U8, name="w_scales", align_bytes=64)
             nc.vector.quantize_mx(words[:].bitcast(FP8X4), scales[:], staged[:])
-            w_coded[e, which, g] = (words, scales)
+            w_coded[i, g] = (words, scales)
 
         def products(e, which):
             bank = psum.tile([P, 4 * C], F32, name=("bank_a", "bank_u")[which])
@@ -118,25 +116,19 @@ def tile_moe_res_glu_sigmoid_kernel(tc, xT, xr, w1, w3, w2, gate, offs, out):
             for t in range(4):
                 chans = slice(t * P, (t + 1) * P)
                 for g in range(PASSES):
-                    words, scales = w_coded[e, which, g]
+                    words, scales = w_coded[2 * e + which, g]
                     nc.tensor.matmul_mx(
                         bank[:, t * C : (t + 1) * C],
                         lhsT=words[:, chans].bitcast(FP8X4),
                         lhsT_scale=scales[:, chans],
                         rhs=g_words[g][:, cols].bitcast(FP8X4),
-                        rhs_scale=g_bytes[g][:, cols],
+                        rhs_scale=g_bytes[4 * g :, cols],
                         start=(g == 0),
                         stop=(g == PASSES - 1),
                     )
             return bank
 
-        def gather_words(g):
-            nc.vector.tensor_copy(g_words[g][:], x_words[g][:].indirect(slots[:]))
-
-        def gather_bytes(g):
-            nc.vector.tensor_copy(g_bytes[g][:], x_bytes[g][:].indirect(slots[:]))
-
-        sig, gated, h_coded, w2_coded, ys, bank_u = {}, {}, {}, {}, {}, {}
+        sig, gated, h_coded, bank_u = {}, {}, {}, {}
 
         def first(e):
             bank = products(e, 0)
@@ -161,36 +153,40 @@ def tile_moe_res_glu_sigmoid_kernel(tc, xT, xr, w1, w3, w2, gate, offs, out):
             nc.vector.quantize_mx(words[:].bitcast(FP8X4), scales[:], gated[e][:])
             h_coded[e] = (words, scales)
 
-        w2_staged = {}
+        def interleave_w2(es):
+            dst = w2_staged[:, es].rearrange("p e (c i j) -> p e c j i", i=4, j=PACK)
+            nc.scalar.copy(dst, w2_raw[:, es].rearrange("p e j (c i) -> p e c j i", i=4))
 
-        def interleave_w2(e):
-            w2_staged[e] = small.tile([P, N * PACK], BF16, name="w2_staged", align_bytes=64)
-            dst = w2_staged[e][:].rearrange("p (c i j) -> p c j i", i=4, j=PACK)
-            nc.scalar.copy(dst, w2_raw[:, e].rearrange("p j (c i) -> p c j i", i=4))
+        def quantize_w2(start, stop):
+            cols = slice(start * N, stop * N)
+            nc.vector.quantize_mx(
+                w2_words[:, cols].bitcast(FP8X4),
+                w2_scales[:, cols],
+                w2_staged[:, start:stop].rearrange("p e c -> p (e c)"),
+            )
 
-        def quantize_w2(e):
-            words = small.tile([P, N], U32, name="w2_words", align_bytes=64)
-            scales = small.tile([P, N], U8, name="w2_scales", align_bytes=64)
-            nc.vector.quantize_mx(words[:].bitcast(FP8X4), scales[:], w2_staged[e][:])
-            w2_coded[e] = (words, scales)
+        bank_y = {}
 
         def down(e):
-            bank = psum.tile([P, C], F32, name="bank_y")
+            bank_y[e] = psum.tile([P, C], F32, name="bank_y")
+            cols = slice(e * N, (e + 1) * N)
             nc.tensor.matmul_mx(
-                bank[:],
-                lhsT=w2_coded[e][0][:].bitcast(FP8X4),
-                lhsT_scale=w2_coded[e][1][:],
+                bank_y[e][:],
+                lhsT=w2_words[:, cols].bitcast(FP8X4),
+                lhsT_scale=w2_scales[:, cols],
                 rhs=h_coded[e][0][:].bitcast(FP8X4),
                 rhs_scale=h_coded[e][1][:],
                 start=True,
                 stop=True,
             )
-            ys[e] = small.tile([P, C], F32, name="y")
-            nc.scalar.copy(ys[e][:], bank[:])
+
+        def weigh(e):
+            cols = slice(e * C, (e + 1) * C)
+            nc.vector.tensor_tensor(weighted[:, cols], bank_y[e][:], gates[:, cols], MULT)
 
         def scatter(e):
             window = scattered[:].indirect(slots[:, e * LIST_COLUMNS : (e + 1) * LIST_COLUMNS])
-            nc.vector.tensor_tensor(window, ys[e][:], gates[:, e * C : (e + 1) * C], MULT)
+            nc.vector.tensor_copy(window, weighted[:, e * C : (e + 1) * C])
 
         last_x = None
         for i in range(len(X_PIECES)):
@@ -199,41 +195,46 @@ def tile_moe_res_glu_sigmoid_kernel(tc, xT, xr, w1, w3, w2, gate, offs, out):
                 quantize_x(*last_x)
             last_x = (i, staged)
             if i == 4:
-                gather_words(0)
-                gather_bytes(0)
+                nc.vector.tensor_copy(g_words[0][:], x_words[0][:].indirect(slots[:]))
         pending = None
-        for k in range(16):
-            e, which, g = k // 4, (k // 2) % 2, k % 2
-            step = k % 4
+        for k in range(4 * E):
+            e, step = k // 4, k % 4
+            i, g = k // 2, k % 2
             if k > 1:
                 quantize_w(*pending)
-            staged = interleave_w(e, which, g, M_VECTOR_LAST if k == 15 else M_VECTOR)
+            staged = interleave_w(i, g, T_VECTOR_LAST if k == 4 * E - 1 else T_VECTOR)
             if k == 0:
                 quantize_x(*last_x)
-                gather_words(1)
+                nc.vector.tensor_copy(g_bytes[:], x_bytes[:].indirect(slots[:]))
             if k == 1:
                 quantize_w(*pending)
-                gather_bytes(1)
+                nc.vector.tensor_copy(g_words[1][:], x_words[1][:].indirect(slots[:]))
             if step == 3:
                 first(e)
             if e > 0 and step == 0:
                 second(e - 1)
-                interleave_w2(e - 1)
+                if e == 1:
+                    interleave_w2(slice(0, E - 1))
                 gating(e - 1)
             if e > 0 and step == 1:
                 quantize_h(e - 1)
-                quantize_w2(e - 1)
+                if e == 1:
+                    quantize_w2(0, 2)
+                    quantize_w2(2, 3)
                 down(e - 1)
+            if e > 0 and step == 2:
+                weigh(e - 1)
                 scatter(e - 1)
-            pending = (e, which, g, staged)
+            pending = (i, g, staged)
         e = E - 1
         quantize_w(*pending)
-        interleave_w2(e)
+        interleave_w2(slice(e, E))
         second(e)
-        quantize_w2(e)
+        quantize_w2(e, E)
         gating(e)
         quantize_h(e)
         down(e)
+        weigh(e)
         scatter(e)
         for start, width in OUT_PIECES:
             cols = slice(start, start + width)

@@ -17,145 +17,162 @@ ADD, MULT = mybir.AluOpType.add, mybir.AluOpType.mult
 P = 128
 PACK = 4
 PASSES = K // (P * PACK)
-X_PIECES = ((0, 0, 256), (0, 256, 256), (0, 512, 512), (1, 0, 512), (1, 512, 512))
-X_VECTOR = 4 / 16
-T_VECTOR = 2
-T_VECTOR_LAST = 3
-OUT_PIECES = ((0, 512), (512, 256), (768, 256))
+TILES = H // P
 LIST_COLUMNS = C // 16
+SCALE_ROW = 4
+
+X_PIECES = ((0, 0, 256), (0, 256, 256), (0, 512, 512), (1, 0, 512), (1, 512, 512))
+X_VECTOR = 1 / 4
+
+COPIERS = "SSTV" "SSTV" "SSTV" "STSV"
+CHUNKS = len(COPIERS)
+OUT_PIECES = ((0, 512), (512, 256), (768, 256))
 
 
 def tile_moe_res_glu_sigmoid_kernel(tc, xT, xr, w1, w3, w2, gate, offs, out):
     nc = tc.nc
     with ExitStack() as ctx:
         keep = ctx.enter_context(tc.tile_pool(name="keep", bufs=1))
-        xpool = ctx.enter_context(tc.tile_pool(name="xpool", bufs=2))
-        wraw = ctx.enter_context(tc.tile_pool(name="wraw", bufs=12))
-        stage = ctx.enter_context(tc.tile_pool(name="stage", bufs=3))
-        coded = ctx.enter_context(tc.tile_pool(name="coded", bufs=8))
-        small = ctx.enter_context(tc.tile_pool(name="small", bufs=2))
+        x_stage = ctx.enter_context(tc.tile_pool(name="x_stage", bufs=2))
+        w_raw = ctx.enter_context(tc.tile_pool(name="w_raw", bufs=12))
+        w_stage = ctx.enter_context(tc.tile_pool(name="w_stage", bufs=4))
+        w_coded = ctx.enter_context(tc.tile_pool(name="w_coded", bufs=8))
+        hidden = ctx.enter_context(tc.tile_pool(name="hidden", bufs=2))
         psum = ctx.enter_context(tc.psum_pool(name="psum", bufs=2))
 
         slots = keep.tile([P, E * LIST_COLUMNS], U16, name="slots")
         x_words = [keep.tile([P, T], U32, name=f"x_words{g}", align_bytes=64) for g in range(PASSES)]
-        x_bytes = keep.tile([P, T], U8, name="x_bytes", align_bytes=64)
-        g_words = [keep.tile([P, E * C], U32, name=f"g_words{g}", align_bytes=64) for g in range(PASSES)]
-        g_bytes = keep.tile([P, E * C], U8, name="g_bytes", align_bytes=64)
-        scattered = keep.tile([P, T], F32, name="scattered")
-        residual = keep.tile([P, T], F32, name="residual")
-        gates = keep.tile([P, E * C], F32, name="gates")
-        w2_raw = keep.tile([P, E, PACK, N], F32, name="w2_raw")
-        w2_staged = keep.tile([P, E, N * PACK], BF16, name="w2_staged", align_bytes=64)
+        x_scales = keep.tile([P, T], U8, name="x_scales", align_bytes=64)
+        slot_words = [keep.tile([P, E * C], U32, name=f"slot_words{g}", align_bytes=64) for g in range(PASSES)]
+        slot_scales = keep.tile([P, E * C], U8, name="slot_scales", align_bytes=64)
         w2_words = keep.tile([P, E * N], U32, name="w2_words", align_bytes=64)
         w2_scales = keep.tile([P, E * N], U8, name="w2_scales", align_bytes=64)
+        w2_staged = keep.tile([P, E, N * PACK], BF16, name="w2_staged", align_bytes=64)
         weighted = keep.tile([P, E * C], F32, name="weighted")
+        scattered = keep.tile([P, T], F32, name="scattered")
+        residual = keep.tile([P, T], F32, name="residual")
         result = keep.tile([P, T], F32, name="result")
-        warm = keep.tile([P, 8], F32, name="warm")
 
+        warm = keep.tile([P, 8], F32, name="warm")
         nc.vector.memset(warm[:], 0.0)
         nc.scalar.activation(warm[:], warm[:], SIGMOID)
-        nc.gpsimd.memset(x_bytes[:], 0)
+        nc.gpsimd.memset(x_scales[:], 0)
         nc.gpsimd.memset(scattered[:], 0.0)
 
         x_rows = xT.rearrange("(g p j) t -> g p j t", g=PASSES, j=PACK)
-        x_raw = {}
+        x_raw = []
         for i, (g, start, width) in enumerate(X_PIECES):
-            x_raw[i] = keep.tile([P, PACK, width], F32, name=f"x_raw{i}")
+            x_raw.append(keep.tile([P, PACK, width], F32, name=f"x_raw{i}"))
             nc.sync.dma_start(x_raw[i][:], x_rows[g, :, :, start : start + width])
             if i == 0:
                 nc.sync.dma_start(slots[:], offs)
 
         w2_rows = w2.rearrange("e (p j) n -> p e j n", j=PACK)
-        w_raw = {}
-        for i in range(2 * E):
-            e, which = i // 2, i % 2
-            rows = (w1, w3)[which][e].rearrange("(g p j) c -> g p j c", g=PASSES, j=PACK)
-            for g in range(PASSES):
-                w_raw[i, g] = wraw.tile([P, PACK, H], F32, name="w_raw")
-                nc.sync.dma_start(w_raw[i, g][:], rows[g])
-            if i == 1:
-                nc.sync.dma_start(w2_raw[:, : E - 1], w2_rows[:, : E - 1])
-                nc.sync.dma_start(gates[:], gate)
-        nc.sync.dma_start(w2_raw[:, E - 1], w2_rows[:, E - 1])
+        w2_raw = keep.tile([P, E - 1, PACK, N], F32, name="w2_raw")
+        w2_raw_last = keep.tile([P, 1, PACK, N], F32, name="w2_raw_last")
+        gates = [keep.tile([P, 2 * C], F32, name=f"gates{half}") for half in range(2)]
+        chunk_raw = []
+        for k in range(CHUNKS):
+            e, which, g = k // 4, k // 2 % 2, k % 2
+            rows = (w1, w3)[which][e].rearrange("(g p j) c -> g p j c", g=PASSES, j=PACK)[g]
+            chunk_raw.append(w_raw.tile([P, PACK, H], F32, name="chunk_raw"))
+            width = H // 2 if k == CHUNKS - 1 else H
+            for c in range(0, H, width):
+                nc.sync.dma_start(chunk_raw[k][:, :, c : c + width], rows[:, :, c : c + width])
+            if k == 3:
+                nc.sync.dma_start(w2_raw[:], w2_rows[:, : E - 1])
+                nc.sync.dma_start(gates[0][:], gate[:, : 2 * C])
+        nc.sync.dma_start(gates[1][:], gate[:, 2 * C :])
+        nc.sync.dma_start(w2_raw_last[:], w2_rows[:, E - 1 :])
         nc.sync.dma_start(residual[:], xr)
 
-        def interleave_x(i):
+        def lay_out_x(i):
             width = X_PIECES[i][2]
-            staged = xpool.tile([P, width * PACK], BF16, name="x_staged", align_bytes=64)
+            staged = x_stage.tile([P, width * PACK], BF16, name="x_staged", align_bytes=64)
             dst = staged[:].rearrange("p (c i j) -> p c j i", i=4, j=PACK)
-            source = x_raw[i][:].rearrange("p j (c i) -> p c j i", i=4)
+            src = x_raw[i][:].rearrange("p j (c i) -> p c j i", i=4)
             cut = int(width * X_VECTOR) // 4
-            nc.vector.tensor_copy(dst[:, :cut], source[:, :cut])
-            nc.scalar.copy(dst[:, cut:], source[:, cut:])
+            nc.vector.tensor_copy(dst[:, :cut], src[:, :cut])
+            nc.scalar.copy(dst[:, cut:], src[:, cut:])
             return staged
 
         def quantize_x(i, staged):
             g, start, width = X_PIECES[i]
             cols = slice(start, start + width)
-            nc.vector.quantize_mx(x_words[g][:, cols].bitcast(FP8X4), x_bytes[4 * g :, cols], staged[:])
+            nc.vector.quantize_mx(x_words[g][:, cols].bitcast(FP8X4), x_scales[SCALE_ROW * g :, cols], staged[:])
 
-        w_coded = {}
+        def gather(slot_tile, token_tile):
+            nc.vector.tensor_copy(slot_tile[:], token_tile[:].indirect(slots[:]))
 
-        def interleave_w(i, g, cut):
-            staged = stage.tile([P, H * PACK], BF16, name="w_staged", align_bytes=64)
-            dst = staged[:].rearrange("p (t m j) -> p m j t", t=4, j=PACK)
-            source = w_raw[i, g][:].rearrange("p j (m t) -> p m j t", t=4)
-            nc.vector.tensor_copy(dst[:, :, :, :cut], source[:, :, :, :cut])
-            nc.scalar.copy(dst[:, :, :, cut:], source[:, :, :, cut:])
+        def lay_out_w(k):
+            staged = w_stage.tile([P, H * PACK], BF16, name="w_staged", align_bytes=64)
+            dst = staged[:].rearrange("p (t m j) -> p m j t", t=TILES, j=PACK)
+            src = chunk_raw[k][:].rearrange("p j (m t) -> p m j t", t=TILES)
+            if COPIERS[k] == "S":
+                nc.scalar.copy(dst, src)
+            elif COPIERS[k] == "T":
+                nc.vector.tensor_copy(dst[:, :, :, :2], src[:, :, :, :2])
+                nc.scalar.copy(dst[:, :, :, 2:], src[:, :, :, 2:])
+            else:
+                rows = P // 2 if k == CHUNKS - 1 else P
+                for m in range(0, P, rows):
+                    nc.vector.tensor_copy(dst[:, m : m + rows], src[:, m : m + rows])
             return staged
 
-        def quantize_w(i, g, staged):
-            words = coded.tile([P, H], U32, name="w_words", align_bytes=64)
-            scales = coded.tile([P, H], U8, name="w_scales", align_bytes=64)
-            nc.vector.quantize_mx(words[:].bitcast(FP8X4), scales[:], staged[:])
-            w_coded[i, g] = (words, scales)
+        coded = {}
 
-        def products(e, which):
-            bank = psum.tile([P, 4 * C], F32, name=("bank_a", "bank_u")[which])
+        def quantize_w(k, staged):
+            words = w_coded.tile([P, H], U32, name="w_words", align_bytes=64)
+            scales = w_coded.tile([P, H], U8, name="w_scales", align_bytes=64)
+            nc.vector.quantize_mx(words[:].bitcast(FP8X4), scales[:], staged[:])
+            coded[k] = (words, scales)
+
+        def products(bank, e, first_chunk):
             cols = slice(e * C, (e + 1) * C)
-            for t in range(4):
-                chans = slice(t * P, (t + 1) * P)
+            for t in range(TILES):
+                channels = slice(t * P, (t + 1) * P)
                 for g in range(PASSES):
-                    words, scales = w_coded[2 * e + which, g]
+                    words, scales = coded[first_chunk + g]
                     nc.tensor.matmul_mx(
                         bank[:, t * C : (t + 1) * C],
-                        lhsT=words[:, chans].bitcast(FP8X4),
-                        lhsT_scale=scales[:, chans],
-                        rhs=g_words[g][:, cols].bitcast(FP8X4),
-                        rhs_scale=g_bytes[4 * g :, cols],
+                        lhsT=words[:, channels].bitcast(FP8X4),
+                        lhsT_scale=scales[:, channels],
+                        rhs=slot_words[g][:, cols].bitcast(FP8X4),
+                        rhs_scale=slot_scales[SCALE_ROW * g :, cols],
                         start=(g == 0),
                         stop=(g == PASSES - 1),
                     )
-            return bank
 
-        sig, gated, h_coded, bank_u = {}, {}, {}, {}
+        sig, bank_b, gated, h_coded, bank_y = {}, {}, {}, {}, {}
 
-        def first(e):
-            bank = products(e, 0)
-            sig[e] = small.tile([P, 4 * C], F32, name="sig")
-            nc.scalar.activation(sig[e][:], bank[:], SIGMOID)
+        def sigmoid_of_a(e):
+            bank_a = psum.tile([P, TILES * C], F32, name="bank_a")
+            products(bank_a, e, 4 * e)
+            sig[e] = hidden.tile([P, TILES * C], F32, name="sig")
+            nc.scalar.activation(sig[e][:], bank_a[:], SIGMOID)
 
-        def second(e):
-            bank_u[e] = products(e, 1)
+        def product_b(e):
+            bank_b[e] = psum.tile([P, TILES * C], F32, name="bank_b")
+            products(bank_b[e], e, 4 * e + 2)
 
-        def gating(e):
-            gated[e] = small.tile([P, 4 * C], BF16, name="gated", align_bytes=64)
+        def make_h(e):
+            gated[e] = hidden.tile([P, C * TILES], BF16, name="gated", align_bytes=64)
             nc.vector.tensor_tensor(
-                gated[e][:].rearrange("p (n t) -> p n t", t=4),
-                bank_u[e][:].rearrange("p (t n) -> p n t", t=4),
-                sig[e][:].rearrange("p (t n) -> p n t", t=4),
+                gated[e][:].rearrange("p (n t) -> p n t", t=TILES),
+                bank_b[e][:].rearrange("p (t n) -> p n t", t=TILES),
+                sig[e][:].rearrange("p (t n) -> p n t", t=TILES),
                 MULT,
             )
 
         def quantize_h(e):
-            words = small.tile([P, C], U32, name="h_words", align_bytes=64)
-            scales = small.tile([P, C], U8, name="h_scales", align_bytes=64)
+            words = hidden.tile([P, C], U32, name="h_words", align_bytes=64)
+            scales = hidden.tile([P, C], U8, name="h_scales", align_bytes=64)
             nc.vector.quantize_mx(words[:].bitcast(FP8X4), scales[:], gated[e][:])
             h_coded[e] = (words, scales)
 
-        def interleave_w2(es):
-            dst = w2_staged[:, es].rearrange("p e (c i j) -> p e c j i", i=4, j=PACK)
-            nc.scalar.copy(dst, w2_raw[:, es].rearrange("p e j (c i) -> p e c j i", i=4))
+        def lay_out_w2(raw, start, stop):
+            dst = w2_staged[:, start:stop].rearrange("p e (c i j) -> p e c j i", i=4, j=PACK)
+            nc.scalar.copy(dst, raw.rearrange("p e j (c i) -> p e c j i", i=4))
 
         def quantize_w2(start, stop):
             cols = slice(start * N, stop * N)
@@ -165,77 +182,75 @@ def tile_moe_res_glu_sigmoid_kernel(tc, xT, xr, w1, w3, w2, gate, offs, out):
                 w2_staged[:, start:stop].rearrange("p e c -> p (e c)"),
             )
 
-        bank_y = {}
-
-        def down(e):
+        def product_y(e):
             bank_y[e] = psum.tile([P, C], F32, name="bank_y")
             cols = slice(e * N, (e + 1) * N)
+            words, scales = h_coded[e]
             nc.tensor.matmul_mx(
                 bank_y[e][:],
                 lhsT=w2_words[:, cols].bitcast(FP8X4),
                 lhsT_scale=w2_scales[:, cols],
-                rhs=h_coded[e][0][:].bitcast(FP8X4),
-                rhs_scale=h_coded[e][1][:],
+                rhs=words[:].bitcast(FP8X4),
+                rhs_scale=scales[:],
                 start=True,
                 stop=True,
             )
 
-        def weigh(e):
+        def weigh_and_scatter(e):
             cols = slice(e * C, (e + 1) * C)
-            nc.vector.tensor_tensor(weighted[:, cols], bank_y[e][:], gates[:, cols], MULT)
-
-        def scatter(e):
+            in_half = slice(e % 2 * C, (e % 2 + 1) * C)
+            nc.vector.tensor_tensor(weighted[:, cols], bank_y[e][:], gates[e // 2][:, in_half], MULT)
             window = scattered[:].indirect(slots[:, e * LIST_COLUMNS : (e + 1) * LIST_COLUMNS])
-            nc.vector.tensor_copy(window, weighted[:, e * C : (e + 1) * C])
+            nc.vector.tensor_copy(window, weighted[:, cols])
 
-        last_x = None
+        staged_before = None
         for i in range(len(X_PIECES)):
-            staged = interleave_x(i)
-            if last_x:
-                quantize_x(*last_x)
-            last_x = (i, staged)
-            if i == 4:
-                nc.vector.tensor_copy(g_words[0][:], x_words[0][:].indirect(slots[:]))
-        pending = None
-        for k in range(4 * E):
+            staged = lay_out_x(i)
+            if i > 0:
+                quantize_x(i - 1, staged_before)
+            staged_before = staged
+        gather(slot_words[0], x_words[0])
+        last_x_staged = staged_before
+
+        for k in range(CHUNKS):
             e, step = k // 4, k % 4
-            i, g = k // 2, k % 2
             if k > 1:
-                quantize_w(*pending)
-            staged = interleave_w(i, g, T_VECTOR_LAST if k == 4 * E - 1 else T_VECTOR)
+                quantize_w(k - 1, staged_before)
+            staged = lay_out_w(k)
             if k == 0:
-                quantize_x(*last_x)
-                nc.vector.tensor_copy(g_bytes[:], x_bytes[:].indirect(slots[:]))
+                quantize_x(len(X_PIECES) - 1, last_x_staged)
+                gather(slot_scales, x_scales)
             if k == 1:
-                quantize_w(*pending)
-                nc.vector.tensor_copy(g_words[1][:], x_words[1][:].indirect(slots[:]))
+                quantize_w(0, staged_before)
+                gather(slot_words[1], x_words[1])
+            staged_before = staged
             if step == 3:
-                first(e)
+                sigmoid_of_a(e)
             if e > 0 and step == 0:
-                second(e - 1)
+                product_b(e - 1)
                 if e == 1:
-                    interleave_w2(slice(0, E - 1))
-                gating(e - 1)
+                    lay_out_w2(w2_raw[:, :2], 0, 2)
+                if e == 2:
+                    lay_out_w2(w2_raw[:, 2:], 2, 3)
+                make_h(e - 1)
             if e > 0 and step == 1:
                 quantize_h(e - 1)
                 if e == 1:
                     quantize_w2(0, 2)
+                if e == 2:
                     quantize_w2(2, 3)
-                down(e - 1)
+                product_y(e - 1)
             if e > 0 and step == 2:
-                weigh(e - 1)
-                scatter(e - 1)
-            pending = (i, g, staged)
-        e = E - 1
-        quantize_w(*pending)
-        interleave_w2(slice(e, E))
-        second(e)
-        quantize_w2(e, E)
-        gating(e)
-        quantize_h(e)
-        down(e)
-        weigh(e)
-        scatter(e)
+                weigh_and_scatter(e - 1)
+
+        quantize_w(CHUNKS - 1, staged_before)
+        product_b(E - 1)
+        lay_out_w2(w2_raw_last[:], E - 1, E)
+        quantize_w2(E - 1, E)
+        make_h(E - 1)
+        quantize_h(E - 1)
+        product_y(E - 1)
+        weigh_and_scatter(E - 1)
         for start, width in OUT_PIECES:
             cols = slice(start, start + width)
             nc.vector.tensor_tensor(result[:, cols], scattered[:, cols], residual[:, cols], ADD)

@@ -21,8 +21,9 @@ TILES = H // P
 LIST_COLUMNS = C // 16
 SCALE_ROW = 4
 
-X_PIECES = ((0, 0, 256), (0, 256, 256), (0, 512, 512), (1, 0, 512), (1, 512, 512))
-X_VECTOR = 1 / 4
+X_PIECE = T // 2
+X_PIECES = ((0, 0), (0, X_PIECE), (1, 0), (1, X_PIECE))
+X_CUT = X_PIECE // 2
 
 COPIERS = "SSTV" "SSTV" "SSTV" "STSV"
 CHUNKS = len(COPIERS)
@@ -60,11 +61,10 @@ def tile_moe_res_glu_sigmoid_kernel(tc, xT, xr, w1, w3, w2, gate, offs, out):
         nc.gpsimd.memset(scattered[:], 0.0)
 
         x_rows = xT.rearrange("(g p j) t -> g p j t", g=PASSES, j=PACK)
-        x_raw = []
-        for i, (g, start, width) in enumerate(X_PIECES):
-            x_raw.append(keep.tile([P, PACK, width], F32, name=f"x_raw{i}"))
-            nc.sync.dma_start(x_raw[i][:], x_rows[g, :, :, start : start + width])
-            if i == 0:
+        x_raw = [keep.tile([P, PACK, T], F32, name=f"x_raw{g}") for g in range(PASSES)]
+        for g in range(PASSES):
+            nc.sync.dma_start(x_raw[g][:], x_rows[g])
+            if g == 0:
                 nc.sync.dma_start(slots[:], offs)
 
         w2_rows = w2.rearrange("e (p j) n -> p e j n", j=PACK)
@@ -87,18 +87,18 @@ def tile_moe_res_glu_sigmoid_kernel(tc, xT, xr, w1, w3, w2, gate, offs, out):
         nc.sync.dma_start(residual[:], xr)
 
         def lay_out_x(i):
-            width = X_PIECES[i][2]
-            staged = x_stage.tile([P, width * PACK], BF16, name="x_staged", align_bytes=64)
+            g, start = X_PIECES[i]
+            staged = x_stage.tile([P, X_PIECE * PACK], BF16, name="x_staged", align_bytes=64)
             dst = staged[:].rearrange("p (c i j) -> p c j i", i=4, j=PACK)
-            src = x_raw[i][:].rearrange("p j (c i) -> p c j i", i=4)
-            cut = int(width * X_VECTOR) // 4
+            src = x_raw[g][:, :, start : start + X_PIECE].rearrange("p j (c i) -> p c j i", i=4)
+            cut = X_CUT // 4
             nc.vector.tensor_copy(dst[:, :cut], src[:, :cut])
             nc.scalar.copy(dst[:, cut:], src[:, cut:])
             return staged
 
         def quantize_x(i, staged):
-            g, start, width = X_PIECES[i]
-            cols = slice(start, start + width)
+            g, start = X_PIECES[i]
+            cols = slice(start, start + X_PIECE)
             nc.vector.quantize_mx(x_words[g][:, cols].bitcast(FP8X4), x_scales[SCALE_ROW * g :, cols], staged[:])
 
         def gather(slot_tile, token_tile):

from contextlib import ExitStack

import concourse.mybir as mybir

K, T, E, C, H, N = 1024, 1024, 4, 128, 512, 128
FLOPS = 2 * E * C * (2 * K * H + H * N)

F32 = mybir.dt.float32
BF16 = mybir.dt.bfloat16
U32 = mybir.dt.uint32
U16 = mybir.dt.uint16
U8 = mybir.dt.uint8
FP8X4 = mybir.dt.float8_e4m3fn_x4
SIGMOID = mybir.ActivationFunctionType.Sigmoid
ADD, MULT = mybir.AluOpType.add, mybir.AluOpType.mult

P = 128
PACK = 4
PASSES = K // (P * PACK)
TILES = H // P
LIST_COLUMNS = C // 16
SCALE_ROW = 4

X_PIECE = T // 2
X_PIECES = ((0, 0), (0, X_PIECE), (1, 0), (1, X_PIECE))
X_CUT = X_PIECE // 2

COPIERS = "SSTV" "SSTV" "SSTV" "STSV"
CHUNKS = len(COPIERS)
OUT_PIECES = ((0, 512), (512, 256), (768, 256))


def tile_moe_res_glu_sigmoid_kernel(tc, xT, xr, w1, w3, w2, gate, offs, out):
    nc = tc.nc
    with ExitStack() as ctx:
        keep = ctx.enter_context(tc.tile_pool(name="keep", bufs=1))
        x_stage = ctx.enter_context(tc.tile_pool(name="x_stage", bufs=2))
        w_raw = ctx.enter_context(tc.tile_pool(name="w_raw", bufs=12))
        w_stage = ctx.enter_context(tc.tile_pool(name="w_stage", bufs=4))
        w_coded = ctx.enter_context(tc.tile_pool(name="w_coded", bufs=8))
        hidden = ctx.enter_context(tc.tile_pool(name="hidden", bufs=2))
        psum = ctx.enter_context(tc.psum_pool(name="psum", bufs=2))

        slots = keep.tile([P, E * LIST_COLUMNS], U16, name="slots")
        x_words = [keep.tile([P, T], U32, name=f"x_words{g}", align_bytes=64) for g in range(PASSES)]
        x_scales = keep.tile([P, T], U8, name="x_scales", align_bytes=64)
        slot_words = [keep.tile([P, E * C], U32, name=f"slot_words{g}", align_bytes=64) for g in range(PASSES)]
        slot_scales = keep.tile([P, E * C], U8, name="slot_scales", align_bytes=64)
        w2_words = keep.tile([P, E * N], U32, name="w2_words", align_bytes=64)
        w2_scales = keep.tile([P, E * N], U8, name="w2_scales", align_bytes=64)
        w2_staged = keep.tile([P, E, N * PACK], BF16, name="w2_staged", align_bytes=64)
        weighted = keep.tile([P, E * C], F32, name="weighted")
        scattered = keep.tile([P, T], F32, name="scattered")
        residual = keep.tile([P, T], F32, name="residual")
        result = keep.tile([P, T], F32, name="result")

        warm = keep.tile([P, 8], F32, name="warm")
        nc.vector.memset(warm[:], 0.0)
        nc.scalar.activation(warm[:], warm[:], SIGMOID)
        nc.gpsimd.memset(x_scales[:], 0)
        nc.gpsimd.memset(scattered[:], 0.0)

        x_rows = xT.rearrange("(g p j) t -> g p j t", g=PASSES, j=PACK)
        x_raw = [keep.tile([P, PACK, T], F32, name=f"x_raw{g}") for g in range(PASSES)]
        for g in range(PASSES):
            nc.sync.dma_start(x_raw[g][:], x_rows[g])
            if g == 0:
                nc.sync.dma_start(slots[:], offs)

        w2_rows = w2.rearrange("e (p j) n -> p e j n", j=PACK)
        w2_raw = keep.tile([P, E - 1, PACK, N], F32, name="w2_raw")
        w2_raw_last = keep.tile([P, 1, PACK, N], F32, name="w2_raw_last")
        gates = [keep.tile([P, 2 * C], F32, name=f"gates{half}") for half in range(2)]
        chunk_raw = []
        for k in range(CHUNKS):
            e, which, g = k // 4, k // 2 % 2, k % 2
            rows = (w1, w3)[which][e].rearrange("(g p j) c -> g p j c", g=PASSES, j=PACK)[g]
            chunk_raw.append(w_raw.tile([P, PACK, H], F32, name="chunk_raw"))
            width = H // 2 if k == CHUNKS - 1 else H
            for c in range(0, H, width):
                nc.sync.dma_start(chunk_raw[k][:, :, c : c + width], rows[:, :, c : c + width])
            if k == 3:
                nc.sync.dma_start(w2_raw[:], w2_rows[:, : E - 1])
                nc.sync.dma_start(gates[0][:], gate[:, : 2 * C])
        nc.sync.dma_start(gates[1][:], gate[:, 2 * C :])
        nc.sync.dma_start(w2_raw_last[:], w2_rows[:, E - 1 :])
        nc.sync.dma_start(residual[:], xr)

        def lay_out_x(i):
            g, start = X_PIECES[i]
            staged = x_stage.tile([P, X_PIECE * PACK], BF16, name="x_staged", align_bytes=64)
            dst = staged[:].rearrange("p (c i j) -> p c j i", i=4, j=PACK)
            src = x_raw[g][:, :, start : start + X_PIECE].rearrange("p j (c i) -> p c j i", i=4)
            cut = X_CUT // 4
            nc.vector.tensor_copy(dst[:, :cut], src[:, :cut])
            nc.scalar.copy(dst[:, cut:], src[:, cut:])
            return staged

        def quantize_x(i, staged):
            g, start = X_PIECES[i]
            cols = slice(start, start + X_PIECE)
            nc.vector.quantize_mx(x_words[g][:, cols].bitcast(FP8X4), x_scales[SCALE_ROW * g :, cols], staged[:])

        def gather(slot_tile, token_tile):
            nc.vector.tensor_copy(slot_tile[:], token_tile[:].indirect(slots[:]))

        def lay_out_w(k):
            staged = w_stage.tile([P, H * PACK], BF16, name="w_staged", align_bytes=64)
            dst = staged[:].rearrange("p (t m j) -> p m j t", t=TILES, j=PACK)
            src = chunk_raw[k][:].rearrange("p j (m t) -> p m j t", t=TILES)
            if COPIERS[k] == "S":
                nc.scalar.copy(dst, src)
            elif COPIERS[k] == "T":
                nc.vector.tensor_copy(dst[:, :, :, :2], src[:, :, :, :2])
                nc.scalar.copy(dst[:, :, :, 2:], src[:, :, :, 2:])
            else:
                rows = P // 2 if k == CHUNKS - 1 else P
                for m in range(0, P, rows):
                    nc.vector.tensor_copy(dst[:, m : m + rows], src[:, m : m + rows])
            return staged

        coded = {}

        def quantize_w(k, staged):
            words = w_coded.tile([P, H], U32, name="w_words", align_bytes=64)
            scales = w_coded.tile([P, H], U8, name="w_scales", align_bytes=64)
            nc.vector.quantize_mx(words[:].bitcast(FP8X4), scales[:], staged[:])
            coded[k] = (words, scales)

        def products(bank, e, first_chunk):
            cols = slice(e * C, (e + 1) * C)
            for t in range(TILES):
                channels = slice(t * P, (t + 1) * P)
                for g in range(PASSES):
                    words, scales = coded[first_chunk + g]
                    nc.tensor.matmul_mx(
                        bank[:, t * C : (t + 1) * C],
                        lhsT=words[:, channels].bitcast(FP8X4),
                        lhsT_scale=scales[:, channels],
                        rhs=slot_words[g][:, cols].bitcast(FP8X4),
                        rhs_scale=slot_scales[SCALE_ROW * g :, cols],
                        start=(g == 0),
                        stop=(g == PASSES - 1),
                    )

        sig, bank_b, gated, h_coded, bank_y = {}, {}, {}, {}, {}

        def sigmoid_of_a(e):
            bank_a = psum.tile([P, TILES * C], F32, name="bank_a")
            products(bank_a, e, 4 * e)
            sig[e] = hidden.tile([P, TILES * C], F32, name="sig")
            nc.scalar.activation(sig[e][:], bank_a[:], SIGMOID)

        def product_b(e):
            bank_b[e] = psum.tile([P, TILES * C], F32, name="bank_b")
            products(bank_b[e], e, 4 * e + 2)

        def make_h(e):
            gated[e] = hidden.tile([P, C * TILES], BF16, name="gated", align_bytes=64)
            nc.vector.tensor_tensor(
                gated[e][:].rearrange("p (n t) -> p n t", t=TILES),
                bank_b[e][:].rearrange("p (t n) -> p n t", t=TILES),
                sig[e][:].rearrange("p (t n) -> p n t", t=TILES),
                MULT,
            )

        def quantize_h(e):
            words = hidden.tile([P, C], U32, name="h_words", align_bytes=64)
            scales = hidden.tile([P, C], U8, name="h_scales", align_bytes=64)
            nc.vector.quantize_mx(words[:].bitcast(FP8X4), scales[:], gated[e][:])
            h_coded[e] = (words, scales)

        def lay_out_w2(raw, start, stop):
            dst = w2_staged[:, start:stop].rearrange("p e (c i j) -> p e c j i", i=4, j=PACK)
            nc.scalar.copy(dst, raw.rearrange("p e j (c i) -> p e c j i", i=4))

        def quantize_w2(start, stop):
            cols = slice(start * N, stop * N)
            nc.vector.quantize_mx(
                w2_words[:, cols].bitcast(FP8X4),
                w2_scales[:, cols],
                w2_staged[:, start:stop].rearrange("p e c -> p (e c)"),
            )

        def product_y(e):
            bank_y[e] = psum.tile([P, C], F32, name="bank_y")
            cols = slice(e * N, (e + 1) * N)
            words, scales = h_coded[e]
            nc.tensor.matmul_mx(
                bank_y[e][:],
                lhsT=w2_words[:, cols].bitcast(FP8X4),
                lhsT_scale=w2_scales[:, cols],
                rhs=words[:].bitcast(FP8X4),
                rhs_scale=scales[:],
                start=True,
                stop=True,
            )

        def weigh_and_scatter(e):
            cols = slice(e * C, (e + 1) * C)
            in_half = slice(e % 2 * C, (e % 2 + 1) * C)
            nc.vector.tensor_tensor(weighted[:, cols], bank_y[e][:], gates[e // 2][:, in_half], MULT)
            window = scattered[:].indirect(slots[:, e * LIST_COLUMNS : (e + 1) * LIST_COLUMNS])
            nc.vector.tensor_copy(window, weighted[:, cols])

        staged_before = None
        for i in range(len(X_PIECES)):
            staged = lay_out_x(i)
            if i > 0:
                quantize_x(i - 1, staged_before)
            staged_before = staged
        gather(slot_words[0], x_words[0])
        last_x_staged = staged_before

        for k in range(CHUNKS):
            e, step = k // 4, k % 4
            if k > 1:
                quantize_w(k - 1, staged_before)
            staged = lay_out_w(k)
            if k == 0:
                quantize_x(len(X_PIECES) - 1, last_x_staged)
                gather(slot_scales, x_scales)
            if k == 1:
                quantize_w(0, staged_before)
                gather(slot_words[1], x_words[1])
            staged_before = staged
            if step == 3:
                sigmoid_of_a(e)
            if e > 0 and step == 0:
                product_b(e - 1)
                if e == 1:
                    lay_out_w2(w2_raw[:, :2], 0, 2)
                if e == 2:
                    lay_out_w2(w2_raw[:, 2:], 2, 3)
                make_h(e - 1)
            if e > 0 and step == 1:
                quantize_h(e - 1)
                if e == 1:
                    quantize_w2(0, 2)
                if e == 2:
                    quantize_w2(2, 3)
                product_y(e - 1)
            if e > 0 and step == 2:
                weigh_and_scatter(e - 1)

        quantize_w(CHUNKS - 1, staged_before)
        product_b(E - 1)
        lay_out_w2(w2_raw_last[:], E - 1, E)
        quantize_w2(E - 1, E)
        make_h(E - 1)
        quantize_h(E - 1)
        product_y(E - 1)
        weigh_and_scatter(E - 1)
        for start, width in OUT_PIECES:
            cols = slice(start, start + width)
            nc.vector.tensor_tensor(result[:, cols], scattered[:, cols], residual[:, cols], ADD)
            nc.sync.dma_start(out[:, cols], result[:, cols])
